import numpy as np
import ml_dtypes


def mxq(x, axis, fmt="e4m3"):
    dtype, down = {"e4m3": (ml_dtypes.float8_e4m3fn, 7), "e5m2": (ml_dtypes.float8_e5m2, 14)}[fmt]
    v = np.moveaxis(np.asarray(x, np.float32).astype(ml_dtypes.bfloat16).astype(np.float64), axis, -1)
    blocks = v.reshape(v.shape[:-1] + (-1, 32))
    amax = np.abs(blocks).max(-1, keepdims=True)
    byte = np.maximum(np.where(amax > 0, np.frexp(amax)[1] - 1 + 127, 0) - down, 1)
    scale = np.exp2(byte - 127.0)
    codes = (blocks / scale).astype(np.float32).astype(dtype).astype(np.float64)
    return np.moveaxis((codes * scale).reshape(v.shape), -1, axis)


WIDE = False


def mx_kscale(k):
    if not WIDE:
        return np.ones(k)
    levels = np.array([10, -10, 5, -5, 0])
    if k % 512:
        return np.exp2(np.random.permutation(np.resize(levels, k // 32))).repeat(32)
    a = np.empty((k // 512, 16))
    for p in range(k // 512):
        a[p, :8] = np.random.permutation(np.resize(levels, 8))
        for g in range(8):
            far = levels[np.abs(levels - a[p, g]) >= 10]
            a[p, g + 8] = far[np.random.randint(len(far))]
    return np.exp2(a.ravel()).repeat(32)


def f64(x):
    return np.asarray(x).astype(np.float64)


def striped(idx):
    return np.tile(idx.reshape(-1, 16).T, (8, 1)).astype(np.uint16)


def unstriped(offs):
    return offs[:16].T.reshape(-1).astype(np.int64)


def pack_weight(w):
    k, n = w.shape
    w = f64(np.asarray(w, np.float32).astype(ml_dtypes.bfloat16)).reshape(k // 32, 32, n)
    amax = np.abs(w).max(1)
    byte = np.clip(np.where(amax > 0, np.frexp(amax)[1] - 1 + 127 - 7, 1), 1, 254)
    scaled = (w * np.exp2(127.0 - byte)[:, None, :]).reshape(k, n).astype(np.float32)
    words = np.ascontiguousarray(scaled.reshape(k // 512, 128, 4, n).transpose(0, 1, 3, 2)).astype(ml_dtypes.float8_e4m3fn).view(np.uint8)
    return words, np.ascontiguousarray(byte.astype(np.uint8).reshape(k // 512, 16, n))


def unpack_weight(words, scales):
    g, p, n, _ = words.shape
    vals = np.ascontiguousarray(words).view(ml_dtypes.float8_e4m3fn).astype(np.float64) * np.repeat(np.exp2(scales.astype(np.float64) - 127.0), 8, axis=1)[..., None]
    return vals.transpose(0, 1, 3, 2).reshape(g * 512, n)

def planes(y):
    n, m = y.shape
    v = y.astype(np.float32).astype(ml_dtypes.bfloat16).astype(np.float64).reshape(n // 32, 32, m)
    top = np.abs(v).max(1)
    byte = np.clip(np.where(top > 0, np.frexp(top)[1] - 1 + 127 - 7, 1), 1, 254)
    codes = (v * np.exp2(127.0 - byte)[:, None, :]).reshape(n, m).astype(np.float32).astype(ml_dtypes.float8_e4m3fn).view(np.uint8)
    words = codes.reshape(n // 512, 128, 4, m).transpose(0, 1, 3, 2)
    return np.ascontiguousarray(words), np.ascontiguousarray(byte.astype(np.uint8).reshape(n // 512, 16, m))


K, T, S, H = 512, 2048, 512, 512


def setup_inputs():
    n = np.random.standard_normal
    s = mx_kscale(K)[:, None]
    u = mx_kscale(S)
    packed_xT = pack_weight(n((K, T)) * s)
    return {
        "x_words": packed_xT[0],
        "x_scales": packed_xT[1],
        "wa": (n((K, H)) / np.sqrt(K) / s).astype(np.float32),
        "wb": (n((K, H)) / np.sqrt(K) / s).astype(np.float32),
        "gt": (np.random.uniform(0.5, 1.5, (S, 1)) * u[:, None]).astype(np.float32),
        "gi": (np.random.uniform(0.5, 1.5, (S, 1)) / u[:, None]).astype(np.float32),
        "old": n((H, H)).astype(np.float32),
        "offs": striped(np.random.permutation(T)[:S]),
        "two": striped(np.random.permutation(T)[:S]),
    }


def reference(x_words, x_scales, wa, wb, gt, gi, old, offs, two):
    xq = unpack_weight(x_words, x_scales)[:, unstriped(offs)]
    a = xq.T @ mxq(f64(wa), 0, "e4m3")
    z = f64(gt) * np.tanh(a)
    x_two = unpack_weight(x_words, x_scales)[:, unstriped(two)]
    b = x_two.T @ mxq(f64(wb), 0, "e4m3")
    z2 = f64(gi) * np.tanh(b)
    cv = 0.0625 * ((mxq(z, 0, "e4m3").T @ mxq(z2, 0, "e4m3")))
    out_0 = f64(old) + 0.25 * (cv - f64(old))
    return (out_0,) + planes(out_0)

@@ -1,0 +1,194 @@
+from contextlib import ExitStack
+
+import concourse.mybir as mybir
+
+K, T, S, H = 512, 2048, 512, 512
+FLOPS = 2 * K * S * H * 2 + 2 * S * H * H
+
+F32 = mybir.dt.float32
+BF16 = mybir.dt.bfloat16
+I32 = mybir.dt.int32
+U32 = mybir.dt.uint32
+U16 = mybir.dt.uint16
+U8 = mybir.dt.uint8
+FP8X4 = mybir.dt.float8_e4m3fn_x4
+ACT = mybir.ActivationFunctionType
+ALU = mybir.AluOpType
+
+P = 128
+PACK = 4
+CHUNK = 128
+CHUNKS = H // CHUNK
+HALF = 256
+
+
+def tile_picked_crosscov_tanh_po_kernel(
+    tc, x_words, x_scales, wa, wb, gt, gi, old, offs, two, out_0, out_1, out_2
+):
+    nc = tc.nc
+    with ExitStack() as ctx:
+        held = ctx.enter_context(tc.tile_pool(name="held", bufs=1))
+        psum = ctx.enter_context(tc.psum_pool(name="psum", bufs=1))
+
+        list_a = held.tile([P, S // 16], U16, name="list_a")
+        list_b = held.tile([P, S // 16], U16, name="list_b")
+        scale_table = held.tile([P, T], U8, name="scale_table")
+        nc.vector.memset(scale_table[:].bitcast(I32), 0)
+        nc.sync.dma_start(list_a[:], offs)
+        nc.sync.dma_start(list_b[:], two)
+        for q in range(4):
+            nc.sync.dma_start(
+                scale_table[32 * q : 32 * q + 4, :].bitcast(I32), x_scales[0, 4 * q : 4 * q + 4, :].bitcast(I32)
+            )
+        word_table = held.tile([P, T], U32, name="word_table")
+        nc.sync.dma_start(word_table[:].bitcast(I32), x_words[0].rearrange("p n t -> p (n t)").bitcast(I32))
+
+        def load_weight(w, name):
+            halves = []
+            for h in range(H // HALF):
+                raw = held.tile([P, PACK, HALF], F32, name=f"{name}_raw{h}")
+                nc.sync.dma_start(raw[:], w.rearrange("(p t) c -> p t c", t=PACK)[:, :, h * HALF : (h + 1) * HALF])
+                halves.append(raw)
+            return halves
+
+        wa_raw = load_weight(wa, "wa")
+        wb_raw = load_weight(wb, "wb")
+        gate_a = held.tile([P, PACK], F32, name="gate_a")
+        gate_b = held.tile([P, PACK], F32, name="gate_b")
+        nc.sync.dma_start(gate_a[:], gt.rearrange("(p t) o -> p (t o)", t=PACK))
+        nc.sync.dma_start(gate_b[:], gi.rearrange("(p t) o -> p (t o)", t=PACK))
+        old_rows = held.tile([P, PACK, H], F32, name="old_rows")
+        nc.sync.dma_start(old_rows[:], old.rearrange("(p t) c -> p t c", t=PACK))
+
+        def gather_scales(entries, name):
+            plain = held.tile([P, S], U8, name=f"{name}_plain")
+            nc.vector.tensor_copy(plain[:], scale_table[:].indirect(entries[:]))
+            scales = held.tile([P, S], U8, name=f"{name}_scales", align_bytes=64)
+            nc.vector.tensor_copy(
+                scales[:].rearrange("p (t m) -> p t m", t=PACK), plain[:].rearrange("p (m t) -> p t m", t=PACK)
+            )
+            return scales
+
+        def gather_words(entries, name, tag):
+            words = held.tile([P, S], U32, name=f"{name}_words", tag=tag, align_bytes=64)
+            nc.vector.tensor_copy(words[:].rearrange("p (t m) -> p m t", t=PACK), word_table[:].indirect(entries[:]))
+            return words
+
+        def interleave(rows, name, on_scalar):
+            grouped = held.tile([P, CHUNK, PACK], BF16, name=name, tag=name, align_bytes=64)
+            dst = grouped[:].rearrange("p (c i) t -> p c t i", i=4)
+            src = rows.rearrange("p t (c i) -> p c t i", i=4)
+            if on_scalar:
+                nc.scalar.activation(dst, src, ACT.Copy)
+            else:
+                nc.vector.tensor_copy(dst, src)
+            return grouped
+
+        def quantize(values, width, name):
+            codes = held.tile([P, width], U32, name=f"{name}_codes", align_bytes=64)
+            scales = held.tile([P, width], U8, name=f"{name}_scales", align_bytes=64)
+            nc.vector.quantize_mx(out=codes[:].bitcast(FP8X4), scales=scales[:], in_=values)
+            return codes, scales
+
+        def products(bank, still, moving):
+            for t in range(PACK):
+                cols = slice(t * P, (t + 1) * P)
+                nc.tensor.matmul_mx(
+                    out=bank[:, t, :],
+                    lhsT=still[0][:, cols].bitcast(FP8X4),
+                    lhsT_scale=still[1][:, cols],
+                    rhs=moving[0][:].bitcast(FP8X4),
+                    rhs_scale=moving[1][:],
+                    start=True,
+                    stop=True,
+                )
+
+        def weight_chunk(w_raw, c, name, on_scalar):
+            at = (c * CHUNK) % HALF
+            grouped = interleave(w_raw[c * CHUNK // HALF][:, :, at : at + CHUNK], f"{name}_bf{c}", on_scalar)
+            return quantize(grouped[:].rearrange("p c t -> p (c t)"), CHUNK, f"{name}{c}")
+
+        def project(picked, w_mx, c, name, bank_tag):
+            bank = psum.tile([P, PACK, CHUNK], F32, name=f"{name}_bank{c}", tag=bank_tag)
+            products(bank, picked, w_mx)
+            return bank
+
+        scales_a = gather_scales(list_a, "xa")
+        words_a = gather_words(list_a, "xa", "xa_words")
+        scales_b = gather_scales(list_b, "xb")
+        picked_a = (words_a, scales_a)
+        wa_mx = [weight_chunk(wa_raw, c, "wa", True) for c in range(CHUNKS)]
+        picked_b = (gather_words(list_b, "xb", "wa_bf1"), scales_b)
+
+        span = CHUNK // PACK
+        tanh_a = []
+        for c in range(CHUNKS):
+            bank = project(picked_a, wa_mx[c], c, "wa", f"bank{c}")
+            th = held.tile([P, PACK, span, PACK], F32, name=f"tanh_a{c}")
+            nc.scalar.activation(th[:], bank[:].rearrange("p t (m u) -> p u m t", u=PACK), ACT.Tanh)
+            tanh_a.append(th)
+        wb_mx = [weight_chunk(wb_raw, c, "wb", c >= 2) for c in range(CHUNKS)]
+        tanh_b = []
+        for c in range(CHUNKS):
+            bank = project(picked_b, wb_mx[c], c, "wb", f"bank{CHUNKS + c}")
+            th = held.tile([P, CHUNK, PACK], F32, name=f"tanh_b{c}")
+            nc.scalar.activation(th[:], bank[:].rearrange("p t n -> p n t"), ACT.Tanh)
+            tanh_b.append(th)
+
+        z_bf = held.tile([P, PACK, P, PACK], BF16, name="z_bf", align_bytes=64)
+        for c in range(CHUNKS):
+            nc.vector.tensor_tensor(
+                z_bf[:, :, c * span : (c + 1) * span, :],
+                tanh_a[c][:],
+                gate_a[:].unsqueeze(1).unsqueeze(1).broadcast_to([P, PACK, span, PACK]),
+                ALU.mult,
+            )
+        z_mx = quantize(z_bf[:].rearrange("p u m t -> p (u m t)"), H, "z")
+
+        y_codes = held.tile([P, H], U32, name="y_codes", align_bytes=64)
+        y_scales = held.tile([P, H], U8, name="y_scales", align_bytes=64)
+        out_rows = out_0.rearrange("(p t) c -> p t c", t=PACK)
+        out_words = out_1[0].rearrange("p n t -> p (n t)").bitcast(I32)
+
+        def gate_second(c):
+            z2_bf = held.tile([P, CHUNK, PACK], BF16, name=f"z2_bf{c}", align_bytes=64)
+            nc.vector.scalar_tensor_tensor(
+                z2_bf[:], tanh_b[c][:], 1.0 / 64.0, gate_b[:].unsqueeze(1).broadcast_to([P, CHUNK, PACK]), ALU.mult, ALU.mult
+            )
+            return z2_bf
+
+        def second_product(c, z2_bf):
+            z2_mx = quantize(z2_bf[:].rearrange("p c t -> p (c t)"), CHUNK, f"z2_{c}")
+            cov = psum.tile([P, PACK, CHUNK], F32, name=f"cov_bank{c}", tag=f"bank{c}")
+            products(cov, z_mx, z2_mx)
+            return cov
+
+        def blend(c, cov):
+            cols = slice(c * CHUNK, (c + 1) * CHUNK)
+            y = held.tile([P, PACK, CHUNK], F32, name=f"y{c}")
+            nc.vector.scalar_tensor_tensor(y[:], old_rows[:, :, cols], 0.75, cov[:], ALU.mult, ALU.add)
+            nc.sync.dma_start(out_rows[:, :, cols], y[:])
+            return interleave(y[:], f"y_bf{c}", c < CHUNKS - 1)
+
+        def planes(c, y_bf):
+            cols = slice(c * CHUNK, (c + 1) * CHUNK)
+            nc.vector.quantize_mx(
+                out=y_codes[:, cols].bitcast(FP8X4), scales=y_scales[:, cols], in_=y_bf[:].rearrange("p c t -> p (c t)")
+            )
+            nc.sync.dma_start(out_words[:, cols], y_codes[:, cols].bitcast(I32))
+
+        gated, covs, rounded = {}, {}, {}
+        for step in range(CHUNKS + 3):
+            if step < CHUNKS:
+                gated[step] = gate_second(step)
+            if 0 <= step - 2 < CHUNKS:
+                rounded[step - 2] = blend(step - 2, covs[step - 2])
+            if 0 <= step - 1 < CHUNKS:
+                covs[step - 1] = second_product(step - 1, gated[step - 1])
+            if 0 <= step - 3 < CHUNKS:
+                planes(step - 3, rounded[step - 3])
+        for q in range(4):
+            engine = nc.sync if q % 2 else nc.scalar
+            engine.dma_start(
+                out_2[0, 4 * q : 4 * q + 4, :].bitcast(I32), y_scales[32 * q : 32 * q + 4, :].bitcast(I32)
+            )

@@ -1,6 +1,7 @@
 from contextlib import ExitStack
 
 import concourse.mybir as mybir
+from concourse.masks import make_identity
 
 K, T, S, H = 512, 2048, 512, 512
 FLOPS = 2 * K * S * H * 2 + 2 * S * H * H
@@ -20,6 +21,8 @@ PACK = 4
 CHUNK = 128
 CHUNKS = H // CHUNK
 HALF = 256
+RUN = 8
+BANKS = 7
 
 
 def tile_picked_crosscov_tanh_po_kernel(
@@ -40,42 +43,54 @@ def tile_picked_crosscov_tanh_po_kernel(
             nc.sync.dma_start(
                 scale_table[32 * q : 32 * q + 4, :].bitcast(I32), x_scales[0, 4 * q : 4 * q + 4, :].bitcast(I32)
             )
+
+        def load_half(w, h, name):
+            raw = held.tile([P, PACK, HALF], F32, name=f"{name}_raw{h}", align_bytes=64)
+            nc.sync.dma_start(raw[:], w.rearrange("(p t) c -> p t c", t=PACK)[:, :, h * HALF : (h + 1) * HALF])
+            return raw
+
+        wa_raw = [load_half(wa, 0, "wa")]
         word_table = held.tile([P, T], U32, name="word_table")
         nc.sync.dma_start(word_table[:].bitcast(I32), x_words[0].rearrange("p n t -> p (n t)").bitcast(I32))
-
-        def load_weight(w, name):
-            halves = []
-            for h in range(H // HALF):
-                raw = held.tile([P, PACK, HALF], F32, name=f"{name}_raw{h}")
-                nc.sync.dma_start(raw[:], w.rearrange("(p t) c -> p t c", t=PACK)[:, :, h * HALF : (h + 1) * HALF])
-                halves.append(raw)
-            return halves
-
-        wa_raw = load_weight(wa, "wa")
-        wb_raw = load_weight(wb, "wb")
-        gate_a = held.tile([P, PACK], F32, name="gate_a")
-        gate_b = held.tile([P, PACK], F32, name="gate_b")
-        nc.sync.dma_start(gate_a[:], gt.rearrange("(p t) o -> p (t o)", t=PACK))
-        nc.sync.dma_start(gate_b[:], gi.rearrange("(p t) o -> p (t o)", t=PACK))
+        wa_raw.append(load_half(wa, 1, "wa"))
+        gate_rows = held.tile([P, P], F32, name="gate_rows")
+        nc.vector.memset(gate_rows[:], 0.0)
+        for first, gate in ((0, gt), (PACK, gi)):
+            nc.sync.dma_start(
+                gate_rows[first : first + PACK, :].rearrange("t (g r) -> t g r", r=RUN),
+                gate.rearrange("(g t r) o -> t g (r o)", t=PACK, r=RUN),
+            )
+        wb_raw = [load_half(wb, 0, "wb")]
+        wb_raw.append(load_half(wb, 1, "wb"))
         old_rows = held.tile([P, PACK, H], F32, name="old_rows")
         nc.sync.dma_start(old_rows[:], old.rearrange("(p t) c -> p t c", t=PACK))
+
+        identity = held.tile([P, P], F32, name="identity")
+        nc.vector.memset(identity[:], 0.0)
+        make_identity(nc, identity[:], nomemset=True)
 
         def gather_scales(entries, name):
             plain = held.tile([P, S], U8, name=f"{name}_plain")
             nc.vector.tensor_copy(plain[:], scale_table[:].indirect(entries[:]))
+            return plain
+
+        def deal_scales(plain, name):
             scales = held.tile([P, S], U8, name=f"{name}_scales", align_bytes=64)
             nc.vector.tensor_copy(
-                scales[:].rearrange("p (t m) -> p t m", t=PACK), plain[:].rearrange("p (m t) -> p t m", t=PACK)
+                scales[:].bitcast(I32).rearrange("p (t g w) -> p t g w", t=PACK, w=RUN // 4),
+                plain[:].bitcast(I32).rearrange("p (g t w) -> p t g w", t=PACK, w=RUN // 4),
             )
             return scales
 
         def gather_words(entries, name, tag):
             words = held.tile([P, S], U32, name=f"{name}_words", tag=tag, align_bytes=64)
-            nc.vector.tensor_copy(words[:].rearrange("p (t m) -> p m t", t=PACK), word_table[:].indirect(entries[:]))
+            nc.vector.tensor_copy(
+                words[:].rearrange("p (t g r) -> p g t r", t=PACK, r=RUN), word_table[:].indirect(entries[:])
+            )
             return words
 
-        def interleave(rows, name, on_scalar):
-            grouped = held.tile([P, CHUNK, PACK], BF16, name=name, tag=name, align_bytes=64)
+        def interleave(rows, width, name, on_scalar, tag=None):
+            grouped = held.tile([P, width, PACK], BF16, name=name, tag=tag or name, align_bytes=64)
             dst = grouped[:].rearrange("p (c i) t -> p c t i", i=4)
             src = rows.rearrange("p t (c i) -> p c t i", i=4)
             if on_scalar:
@@ -90,59 +105,60 @@ def tile_picked_crosscov_tanh_po_kernel(
             nc.vector.quantize_mx(out=codes[:].bitcast(FP8X4), scales=scales[:], in_=values)
             return codes, scales
 
-        def products(bank, still, moving):
+        def products(bank, still, moving, at):
             for t in range(PACK):
                 cols = slice(t * P, (t + 1) * P)
                 nc.tensor.matmul_mx(
                     out=bank[:, t, :],
                     lhsT=still[0][:, cols].bitcast(FP8X4),
                     lhsT_scale=still[1][:, cols],
-                    rhs=moving[0][:].bitcast(FP8X4),
-                    rhs_scale=moving[1][:],
+                    rhs=moving[0][:, at : at + CHUNK].bitcast(FP8X4),
+                    rhs_scale=moving[1][:, at : at + CHUNK],
                     start=True,
                     stop=True,
                 )
 
-        def weight_chunk(w_raw, c, name, on_scalar):
-            at = (c * CHUNK) % HALF
-            grouped = interleave(w_raw[c * CHUNK // HALF][:, :, at : at + CHUNK], f"{name}_bf{c}", on_scalar)
-            return quantize(grouped[:].rearrange("p c t -> p (c t)"), CHUNK, f"{name}{c}")
+        def weight_piece(raw, at, width, name, on_scalar, tag=None):
+            grouped = interleave(raw[:, :, at : at + width], width, f"{name}_bf", on_scalar, tag)
+            piece = quantize(grouped[:].rearrange("p c t -> p (c t)"), width, name)
+            return [(piece, first) for first in range(0, width, CHUNK)]
 
         def project(picked, w_mx, c, name, bank_tag):
             bank = psum.tile([P, PACK, CHUNK], F32, name=f"{name}_bank{c}", tag=bank_tag)
-            products(bank, picked, w_mx)
+            products(bank, picked, *w_mx[c])
             return bank
 
-        scales_a = gather_scales(list_a, "xa")
-        words_a = gather_words(list_a, "xa", "xa_words")
-        scales_b = gather_scales(list_b, "xb")
-        picked_a = (words_a, scales_a)
-        wa_mx = [weight_chunk(wa_raw, c, "wa", True) for c in range(CHUNKS)]
-        picked_b = (gather_words(list_b, "xb", "wa_bf1"), scales_b)
+        plain_a = gather_scales(list_a, "xa")
+        plain_b = gather_scales(list_b, "xb")
+        scales_a = deal_scales(plain_a, "xa")
+        scales_b = deal_scales(plain_b, "xb")
+        wa_mx = weight_piece(wa_raw[0], 0, CHUNK, "wa0", True) + weight_piece(wa_raw[0], CHUNK, CHUNK, "wa1", True)
+        picked_a = (gather_words(list_a, "xa", "wa0_bf"), scales_a)
+        picked_b = (gather_words(list_b, "xb", "wa1_bf"), scales_b)
+        wa_mx = wa_mx + weight_piece(wa_raw[1], 0, HALF, "wa2", True)
 
         span = CHUNK // PACK
         tanh_a = []
         for c in range(CHUNKS):
-            bank = project(picked_a, wa_mx[c], c, "wa", f"bank{c}")
-            th = held.tile([P, PACK, span, PACK], F32, name=f"tanh_a{c}")
+            bank = project(picked_a, wa_mx, c, "wa", f"bank{c}")
+            th = held.tile([P, PACK, span, PACK], F32, name=f"tanh_a{c}", tag="wa_raw1" if c == 0 else f"tanh_a{c}", align_bytes=64)
             nc.scalar.activation(th[:], bank[:].rearrange("p t (m u) -> p u m t", u=PACK), ACT.Tanh)
             tanh_a.append(th)
-        wb_mx = [weight_chunk(wb_raw, c, "wb", c >= 2) for c in range(CHUNKS)]
-        tanh_b = []
-        for c in range(CHUNKS):
-            bank = project(picked_b, wb_mx[c], c, "wb", f"bank{CHUNKS + c}")
-            th = held.tile([P, CHUNK, PACK], F32, name=f"tanh_b{c}")
-            nc.scalar.activation(th[:], bank[:].rearrange("p t n -> p n t"), ACT.Tanh)
-            tanh_b.append(th)
+        wb_mx = weight_piece(wb_raw[0], 0, HALF, "wb0", False, "wa2_bf")
 
-        z_bf = held.tile([P, PACK, P, PACK], BF16, name="z_bf", align_bytes=64)
+        gate_bank = psum.tile([P, P], F32, name="gate_bank")
+        nc.tensor.transpose(gate_bank[:], gate_rows[:], identity[:])
+        gate_a = gate_bank[:, 0:PACK]
+        gate_b = gate_bank[:, PACK : 2 * PACK]
+        z_bf = held.tile([P, PACK, P, PACK], BF16, name="z_bf", tag="wb_raw0", align_bytes=64)
         for c in range(CHUNKS):
             nc.vector.tensor_tensor(
                 z_bf[:, :, c * span : (c + 1) * span, :],
                 tanh_a[c][:],
-                gate_a[:].unsqueeze(1).unsqueeze(1).broadcast_to([P, PACK, span, PACK]),
+                gate_a.unsqueeze(1).unsqueeze(1).broadcast_to([P, PACK, span, PACK]),
                 ALU.mult,
             )
+        wb_mx = wb_mx + weight_piece(wb_raw[1], 0, HALF, "wb2", True, "wa_raw1")
         z_mx = quantize(z_bf[:].rearrange("p u m t -> p (u m t)"), H, "z")
 
         y_codes = held.tile([P, H], U32, name="y_codes", align_bytes=64)
@@ -150,17 +166,25 @@ def tile_picked_crosscov_tanh_po_kernel(
         out_rows = out_0.rearrange("(p t) c -> p t c", t=PACK)
         out_words = out_1[0].rearrange("p n t -> p (n t)").bitcast(I32)
 
-        def gate_second(c):
+        y_bf = [held.tile([P, HALF, PACK], BF16, name=f"y_bf{h}", align_bytes=64) for h in range(H // HALF)]
+
+        def tanh_second(c):
+            bank = project(picked_b, wb_mx, c, "wb", f"bank{(CHUNKS + c) % BANKS}")
+            th = held.tile([P, CHUNK, PACK], F32, name=f"tanh_b{c}")
+            nc.scalar.activation(th[:], bank[:].rearrange("p t n -> p n t"), ACT.Tanh)
+            return th
+
+        def gate_second(c, th):
             z2_bf = held.tile([P, CHUNK, PACK], BF16, name=f"z2_bf{c}", align_bytes=64)
             nc.vector.scalar_tensor_tensor(
-                z2_bf[:], tanh_b[c][:], 1.0 / 64.0, gate_b[:].unsqueeze(1).broadcast_to([P, CHUNK, PACK]), ALU.mult, ALU.mult
+                z2_bf[:], th[:], 1.0 / 64.0, gate_b.unsqueeze(1).broadcast_to([P, CHUNK, PACK]), ALU.mult, ALU.mult
             )
             return z2_bf
 
         def second_product(c, z2_bf):
             z2_mx = quantize(z2_bf[:].rearrange("p c t -> p (c t)"), CHUNK, f"z2_{c}")
-            cov = psum.tile([P, PACK, CHUNK], F32, name=f"cov_bank{c}", tag=f"bank{c}")
-            products(cov, z_mx, z2_mx)
+            cov = psum.tile([P, PACK, CHUNK], F32, name=f"cov_bank{c}", tag=f"bank{(2 * CHUNKS + c) % BANKS}")
+            products(cov, z_mx, z2_mx, 0)
             return cov
 
         def blend(c, cov):
@@ -168,25 +192,33 @@ def tile_picked_crosscov_tanh_po_kernel(
             y = held.tile([P, PACK, CHUNK], F32, name=f"y{c}")
             nc.vector.scalar_tensor_tensor(y[:], old_rows[:, :, cols], 0.75, cov[:], ALU.mult, ALU.add)
             nc.sync.dma_start(out_rows[:, :, cols], y[:])
-            return interleave(y[:], f"y_bf{c}", c < CHUNKS - 1)
+            at = (c * CHUNK) % HALF
+            dst = y_bf[c * CHUNK // HALF][:, at : at + CHUNK, :].rearrange("p (c i) t -> p c t i", i=4)
+            src = y[:].rearrange("p t (c i) -> p c t i", i=4)
+            if c < CHUNKS - 1:
+                nc.scalar.activation(dst, src, ACT.Copy)
+            else:
+                nc.vector.tensor_copy(dst, src)
 
-        def planes(c, y_bf):
-            cols = slice(c * CHUNK, (c + 1) * CHUNK)
+        def planes(h):
+            cols = slice(h * HALF, (h + 1) * HALF)
             nc.vector.quantize_mx(
-                out=y_codes[:, cols].bitcast(FP8X4), scales=y_scales[:, cols], in_=y_bf[:].rearrange("p c t -> p (c t)")
+                out=y_codes[:, cols].bitcast(FP8X4), scales=y_scales[:, cols], in_=y_bf[h][:].rearrange("p c t -> p (c t)")
             )
             nc.sync.dma_start(out_words[:, cols], y_codes[:, cols].bitcast(I32))
 
-        gated, covs, rounded = {}, {}, {}
-        for step in range(CHUNKS + 3):
-            if step < CHUNKS:
-                gated[step] = gate_second(step)
-            if 0 <= step - 2 < CHUNKS:
-                rounded[step - 2] = blend(step - 2, covs[step - 2])
+        tanh_b, gated, covs = [], [], []
+        for step in range(CHUNKS + 4):
+            if 0 <= step - 0 < CHUNKS:
+                tanh_b.append(tanh_second(step - 0))
+            if 0 <= step - 0 < CHUNKS:
+                gated.append(gate_second(step - 0, tanh_b[step - 0]))
             if 0 <= step - 1 < CHUNKS:
-                covs[step - 1] = second_product(step - 1, gated[step - 1])
+                covs.append(second_product(step - 1, gated[step - 1]))
             if 0 <= step - 3 < CHUNKS:
-                planes(step - 3, rounded[step - 3])
+                blend(step - 3, covs[step - 3])
+            if 0 <= step - 4 < CHUNKS and (step - 4) % 2 == 1:
+                planes((step - 4) // 2)
         for q in range(4):
             engine = nc.sync if q % 2 else nc.scalar
             engine.dma_start(

from contextlib import ExitStack

import concourse.mybir as mybir
from concourse.masks import make_identity

K, T, S, H = 512, 2048, 512, 512
FLOPS = 2 * K * S * H * 2 + 2 * S * H * H

F32 = mybir.dt.float32
BF16 = mybir.dt.bfloat16
I32 = mybir.dt.int32
U32 = mybir.dt.uint32
U16 = mybir.dt.uint16
U8 = mybir.dt.uint8
FP8X4 = mybir.dt.float8_e4m3fn_x4
ACT = mybir.ActivationFunctionType
ALU = mybir.AluOpType

P = 128
PACK = 4
CHUNK = 128
CHUNKS = H // CHUNK
HALF = 256
RUN = 8
BANKS = 7


def tile_picked_crosscov_tanh_po_kernel(
    tc, x_words, x_scales, wa, wb, gt, gi, old, offs, two, out_0, out_1, out_2
):
    nc = tc.nc
    with ExitStack() as ctx:
        held = ctx.enter_context(tc.tile_pool(name="held", bufs=1))
        psum = ctx.enter_context(tc.psum_pool(name="psum", bufs=1))

        list_a = held.tile([P, S // 16], U16, name="list_a")
        list_b = held.tile([P, S // 16], U16, name="list_b")
        scale_table = held.tile([P, T], U8, name="scale_table")
        nc.vector.memset(scale_table[:].bitcast(I32), 0)
        nc.sync.dma_start(list_a[:], offs)
        nc.sync.dma_start(list_b[:], two)
        for q in range(4):
            nc.sync.dma_start(
                scale_table[32 * q : 32 * q + 4, :].bitcast(I32), x_scales[0, 4 * q : 4 * q + 4, :].bitcast(I32)
            )

        def load_half(w, h, name):
            raw = held.tile([P, PACK, HALF], F32, name=f"{name}_raw{h}", align_bytes=64)
            nc.sync.dma_start(raw[:], w.rearrange("(p t) c -> p t c", t=PACK)[:, :, h * HALF : (h + 1) * HALF])
            return raw

        wa_raw = [load_half(wa, 0, "wa")]
        word_table = held.tile([P, T], U32, name="word_table")
        nc.sync.dma_start(word_table[:].bitcast(I32), x_words[0].rearrange("p n t -> p (n t)").bitcast(I32))
        wa_raw.append(load_half(wa, 1, "wa"))
        gate_rows = held.tile([P, P], F32, name="gate_rows")
        nc.vector.memset(gate_rows[:], 0.0)
        for first, gate in ((0, gt), (PACK, gi)):
            nc.sync.dma_start(
                gate_rows[first : first + PACK, :].rearrange("t (g r) -> t g r", r=RUN),
                gate.rearrange("(g t r) o -> t g (r o)", t=PACK, r=RUN),
            )
        wb_raw = [load_half(wb, 0, "wb")]
        wb_raw.append(load_half(wb, 1, "wb"))
        old_rows = held.tile([P, PACK, H], F32, name="old_rows")
        nc.sync.dma_start(old_rows[:], old.rearrange("(p t) c -> p t c", t=PACK))

        identity = held.tile([P, P], F32, name="identity")
        nc.vector.memset(identity[:], 0.0)
        make_identity(nc, identity[:], nomemset=True)

        def gather_scales(entries, name):
            plain = held.tile([P, S], U8, name=f"{name}_plain")
            nc.vector.tensor_copy(plain[:], scale_table[:].indirect(entries[:]))
            return plain

        def deal_scales(plain, name):
            scales = held.tile([P, S], U8, name=f"{name}_scales", align_bytes=64)
            nc.vector.tensor_copy(
                scales[:].bitcast(I32).rearrange("p (t g w) -> p t g w", t=PACK, w=RUN // 4),
                plain[:].bitcast(I32).rearrange("p (g t w) -> p t g w", t=PACK, w=RUN // 4),
            )
            return scales

        def gather_words(entries, name, tag):
            words = held.tile([P, S], U32, name=f"{name}_words", tag=tag, align_bytes=64)
            nc.vector.tensor_copy(
                words[:].rearrange("p (t g r) -> p g t r", t=PACK, r=RUN), word_table[:].indirect(entries[:])
            )
            return words

        def interleave(rows, width, name, on_scalar, tag=None):
            grouped = held.tile([P, width, PACK], BF16, name=name, tag=tag or name, align_bytes=64)
            dst = grouped[:].rearrange("p (c i) t -> p c t i", i=4)
            src = rows.rearrange("p t (c i) -> p c t i", i=4)
            if on_scalar:
                nc.scalar.activation(dst, src, ACT.Copy)
            else:
                nc.vector.tensor_copy(dst, src)
            return grouped

        def quantize(values, width, name):
            codes = held.tile([P, width], U32, name=f"{name}_codes", align_bytes=64)
            scales = held.tile([P, width], U8, name=f"{name}_scales", align_bytes=64)
            nc.vector.quantize_mx(out=codes[:].bitcast(FP8X4), scales=scales[:], in_=values)
            return codes, scales

        def products(bank, still, moving, at):
            for t in range(PACK):
                cols = slice(t * P, (t + 1) * P)
                nc.tensor.matmul_mx(
                    out=bank[:, t, :],
                    lhsT=still[0][:, cols].bitcast(FP8X4),
                    lhsT_scale=still[1][:, cols],
                    rhs=moving[0][:, at : at + CHUNK].bitcast(FP8X4),
                    rhs_scale=moving[1][:, at : at + CHUNK],
                    start=True,
                    stop=True,
                )

        def weight_piece(raw, at, width, name, on_scalar, tag=None):
            grouped = interleave(raw[:, :, at : at + width], width, f"{name}_bf", on_scalar, tag)
            piece = quantize(grouped[:].rearrange("p c t -> p (c t)"), width, name)
            return [(piece, first) for first in range(0, width, CHUNK)]

        def project(picked, w_mx, c, name, bank_tag):
            bank = psum.tile([P, PACK, CHUNK], F32, name=f"{name}_bank{c}", tag=bank_tag)
            products(bank, picked, *w_mx[c])
            return bank

        plain_a = gather_scales(list_a, "xa")
        plain_b = gather_scales(list_b, "xb")
        scales_a = deal_scales(plain_a, "xa")
        scales_b = deal_scales(plain_b, "xb")
        wa_mx = weight_piece(wa_raw[0], 0, CHUNK, "wa0", True) + weight_piece(wa_raw[0], CHUNK, CHUNK, "wa1", True)
        picked_a = (gather_words(list_a, "xa", "wa0_bf"), scales_a)
        picked_b = (gather_words(list_b, "xb", "wa1_bf"), scales_b)
        wa_mx = wa_mx + weight_piece(wa_raw[1], 0, HALF, "wa2", True)

        span = CHUNK // PACK
        tanh_a = []
        for c in range(CHUNKS):
            bank = project(picked_a, wa_mx, c, "wa", f"bank{c}")
            th = held.tile([P, PACK, span, PACK], F32, name=f"tanh_a{c}", tag="wa_raw1" if c == 0 else f"tanh_a{c}", align_bytes=64)
            nc.scalar.activation(th[:], bank[:].rearrange("p t (m u) -> p u m t", u=PACK), ACT.Tanh)
            tanh_a.append(th)
        wb_mx = weight_piece(wb_raw[0], 0, HALF, "wb0", False, "wa2_bf")

        gate_bank = psum.tile([P, P], F32, name="gate_bank")
        nc.tensor.transpose(gate_bank[:], gate_rows[:], identity[:])
        gate_a = gate_bank[:, 0:PACK]
        gate_b = gate_bank[:, PACK : 2 * PACK]
        z_bf = held.tile([P, PACK, P, PACK], BF16, name="z_bf", tag="wb_raw0", align_bytes=64)
        for c in range(CHUNKS):
            nc.vector.tensor_tensor(
                z_bf[:, :, c * span : (c + 1) * span, :],
                tanh_a[c][:],
                gate_a.unsqueeze(1).unsqueeze(1).broadcast_to([P, PACK, span, PACK]),
                ALU.mult,
            )
        wb_mx = wb_mx + weight_piece(wb_raw[1], 0, HALF, "wb2", True, "wa_raw1")
        z_mx = quantize(z_bf[:].rearrange("p u m t -> p (u m t)"), H, "z")

        y_codes = held.tile([P, H], U32, name="y_codes", align_bytes=64)
        y_scales = held.tile([P, H], U8, name="y_scales", align_bytes=64)
        out_rows = out_0.rearrange("(p t) c -> p t c", t=PACK)
        out_words = out_1[0].rearrange("p n t -> p (n t)").bitcast(I32)

        y_bf = [held.tile([P, HALF, PACK], BF16, name=f"y_bf{h}", align_bytes=64) for h in range(H // HALF)]

        def tanh_second(c):
            bank = project(picked_b, wb_mx, c, "wb", f"bank{(CHUNKS + c) % BANKS}")
            th = held.tile([P, CHUNK, PACK], F32, name=f"tanh_b{c}")
            nc.scalar.activation(th[:], bank[:].rearrange("p t n -> p n t"), ACT.Tanh)
            return th

        def gate_second(c, th):
            z2_bf = held.tile([P, CHUNK, PACK], BF16, name=f"z2_bf{c}", align_bytes=64)
            nc.vector.scalar_tensor_tensor(
                z2_bf[:], th[:], 1.0 / 64.0, gate_b.unsqueeze(1).broadcast_to([P, CHUNK, PACK]), ALU.mult, ALU.mult
            )
            return z2_bf

        def second_product(c, z2_bf):
            z2_mx = quantize(z2_bf[:].rearrange("p c t -> p (c t)"), CHUNK, f"z2_{c}")
            cov = psum.tile([P, PACK, CHUNK], F32, name=f"cov_bank{c}", tag=f"bank{(2 * CHUNKS + c) % BANKS}")
            products(cov, z_mx, z2_mx, 0)
            return cov

        def blend(c, cov):
            cols = slice(c * CHUNK, (c + 1) * CHUNK)
            y = held.tile([P, PACK, CHUNK], F32, name=f"y{c}")
            nc.vector.scalar_tensor_tensor(y[:], old_rows[:, :, cols], 0.75, cov[:], ALU.mult, ALU.add)
            nc.sync.dma_start(out_rows[:, :, cols], y[:])
            at = (c * CHUNK) % HALF
            dst = y_bf[c * CHUNK // HALF][:, at : at + CHUNK, :].rearrange("p (c i) t -> p c t i", i=4)
            src = y[:].rearrange("p t (c i) -> p c t i", i=4)
            if c < CHUNKS - 1:
                nc.scalar.activation(dst, src, ACT.Copy)
            else:
                nc.vector.tensor_copy(dst, src)

        def planes(h):
            cols = slice(h * HALF, (h + 1) * HALF)
            nc.vector.quantize_mx(
                out=y_codes[:, cols].bitcast(FP8X4), scales=y_scales[:, cols], in_=y_bf[h][:].rearrange("p c t -> p (c t)")
            )
            nc.sync.dma_start(out_words[:, cols], y_codes[:, cols].bitcast(I32))

        tanh_b, gated, covs = [], [], []
        for step in range(CHUNKS + 4):
            if 0 <= step - 0 < CHUNKS:
                tanh_b.append(tanh_second(step - 0))
            if 0 <= step - 0 < CHUNKS:
                gated.append(gate_second(step - 0, tanh_b[step - 0]))
            if 0 <= step - 1 < CHUNKS:
                covs.append(second_product(step - 1, gated[step - 1]))
            if 0 <= step - 3 < CHUNKS:
                blend(step - 3, covs[step - 3])
            if 0 <= step - 4 < CHUNKS and (step - 4) % 2 == 1:
                planes((step - 4) // 2)
        for q in range(4):
            engine = nc.sync if q % 2 else nc.scalar
            engine.dma_start(
                out_2[0, 4 * q : 4 * q + 4, :].bitcast(I32), y_scales[32 * q : 32 * q + 4, :].bitcast(I32)
            )
